import numpy as np
import ml_dtypes


def mxq(x, axis, fmt="e4m3"):
    dtype, down = {"e4m3": (ml_dtypes.float8_e4m3fn, 7), "e5m2": (ml_dtypes.float8_e5m2, 14)}[fmt]
    v = np.moveaxis(np.asarray(x, np.float32).astype(ml_dtypes.bfloat16).astype(np.float64), axis, -1)
    blocks = v.reshape(v.shape[:-1] + (-1, 32))
    amax = np.abs(blocks).max(-1, keepdims=True)
    byte = np.maximum(np.where(amax > 0, np.frexp(amax)[1] - 1 + 127, 0) - down, 1)
    scale = np.exp2(byte - 127.0)
    codes = (blocks / scale).astype(np.float32).astype(dtype).astype(np.float64)
    return np.moveaxis((codes * scale).reshape(v.shape), -1, axis)


WIDE = False


def mx_kscale(k):
    if not WIDE:
        return np.ones(k)
    levels = np.array([10, -10, 5, -5, 0])
    if k % 512:
        return np.exp2(np.random.permutation(np.resize(levels, k // 32))).repeat(32)
    a = np.empty((k // 512, 16))
    for p in range(k // 512):
        a[p, :8] = np.random.permutation(np.resize(levels, 8))
        for g in range(8):
            far = levels[np.abs(levels - a[p, g]) >= 10]
            a[p, g + 8] = far[np.random.randint(len(far))]
    return np.exp2(a.ravel()).repeat(32)


def f64(x):
    return np.asarray(x).astype(np.float64)


def striped8(idx):
    return np.asarray(idx).reshape(8, -1, 16).transpose(0, 2, 1).reshape(128, -1).astype(np.uint16)


def unstriped8(offs):
    return offs.reshape(8, 16, -1).transpose(0, 2, 1).reshape(8, -1).astype(np.int64)


def pick8(x, idx, run):
    r = np.arange(len(x))
    return x[r[:, None], idx[r % (8 * run) // run]]


E2M1 = np.array([0.0, 0.5, 1.0, 1.5, 2.0, 3.0, 4.0, 6.0, -0.0, -0.5, -1.0, -1.5, -2.0, -3.0, -4.0, -6.0])


def pack_weight(w, fmt):
    k, n = w.shape
    w = f64(np.asarray(w, np.float32).astype(ml_dtypes.bfloat16)).reshape(k // 32, 32, n)
    amax = np.abs(w).max(1)
    if fmt == "e4m3":
        byte = np.frexp(amax)[1] - 1 + 127 - 7
    else:
        mant, ex = np.frexp(amax / 6.0)
        byte = np.where(mant > 0.5, ex, ex - 1) + 127
    byte = np.clip(np.where(amax > 0, byte, 1), 1, 254)
    scaled = (w * np.exp2(127.0 - byte)[:, None, :]).reshape(k, n).astype(np.float32)
    by_word = np.ascontiguousarray(scaled.reshape(k // 512, 128, 4, n).transpose(0, 1, 3, 2))
    if fmt == "e4m3":
        words = by_word.astype(ml_dtypes.float8_e4m3fn).view(np.uint8)
    else:
        c = by_word.astype(ml_dtypes.float4_e2m1fn).view(np.uint8) & 0xF
        words = (c[..., 0::2] | (c[..., 1::2] << 4)).reshape(k // 512, 128, 2 * n)
    return np.ascontiguousarray(words), np.ascontiguousarray(byte.astype(np.uint8).reshape(k // 512, 16, n))


def unpack_weight(words, scales, fmt):
    g, _, n = scales.shape
    words = np.ascontiguousarray(words).reshape(g, 128, n, -1)
    if fmt == "e4m3":
        vals = words.view(ml_dtypes.float8_e4m3fn).astype(np.float64)
    else:
        nib = np.empty((g, 128, n, 4), np.uint8)
        nib[..., 0::2] = words & 0xF
        nib[..., 1::2] = words >> 4
        vals = E2M1[nib]
    vals = vals * np.repeat(np.exp2(scales.astype(np.float64) - 127.0), 8, axis=1)[..., None]
    return vals.transpose(0, 1, 3, 2).reshape(g * 512, n)


K, T, J, N = 512, 512, 512, 512


def setup_inputs():
    n = np.random.standard_normal
    idx = np.stack([np.random.randint(0, T, J) for _ in range(8)])
    idx2 = np.stack([np.random.randint(0, T, J) for _ in range(8)])
    fk = mx_kscale(K)
    xtp = pack_weight(n((K, T)) / fk[:, None], "e4m3")
    wap = pack_weight(n((K, N)) * 1 / np.sqrt(K) * fk[:, None], "e2m1")
    return {
        "xt_words": xtp[0],
        "xt_scales": xtp[1],
        "wa_words": wap[0],
        "wa_scales": wap[1],
        "wb": (n((K, N)) * 1 / np.sqrt(K) * fk[:, None]).astype(np.float32),
        "gm": (np.random.uniform(0.5, 2.0, (N, 1))).astype(np.float32),
        "offs": striped8(idx),
        "offs2": striped8(idx2),
    }


def reference(xt_words, xt_scales, wa_words, wa_scales, wb, gm, offs, offs2):
    idx = unstriped8(offs)
    idx2 = unstriped8(offs2)
    xtu = unpack_weight(xt_words, xt_scales, "e4m3")
    wau = unpack_weight(wa_words, wa_scales, "e2m1")
    z = wau.T @ xtu
    wbq = mxq(f64(wb), 0, "e4m3")
    u = wbq.T @ xtu
    y = f64(gm) * pick8(z, idx, 64) / (1.0 + np.maximum(pick8(u, idx2, 64), 0.0))
    return y

@@ -1,0 +1,135 @@
+from contextlib import ExitStack
+
+import concourse.mybir as mybir
+
+K, T, J, N = 512, 512, 512, 512
+FLOPS = 2 * 2 * K * N * T
+F32 = mybir.dt.float32
+BF16 = mybir.dt.bfloat16
+I32 = mybir.dt.int32
+U32 = mybir.dt.uint32
+U16 = mybir.dt.uint16
+U8 = mybir.dt.uint8
+FP8X4 = mybir.dt.float8_e4m3fn_x4
+FP4X4 = mybir.dt.float4_e2m1fn_x4
+ACT = mybir.ActivationFunctionType
+ALU = mybir.AluOpType
+P = 128
+S = 4
+H = 256
+
+
+def tile_list_head_divided_by_own_list_kernel(tc, xt_words, xt_scales, wa_words, wa_scales, wb, gm, offs, offs2, out):
+    nc = tc.nc
+    with ExitStack() as ctx:
+        keep = ctx.enter_context(tc.tile_pool(name="keep", bufs=1))
+        psum = ctx.enter_context(tc.psum_pool(name="psum", bufs=1))
+
+        list_z = keep.tile([P, J // 16], U16, name="list_z")
+        list_u = keep.tile([P, J // 16], U16, name="list_u")
+        planes = keep.tile([P, T + N], U8, name="planes", align_bytes=64)
+        x_words = keep.tile([P, T], U32, name="x_words", align_bytes=64)
+        a_raw = keep.tile([P, 2 * N], U8, name="a_raw", align_bytes=64)
+        gains = keep.tile([P, S], F32, name="gains")
+        nc.gpsimd.memset(planes[:].bitcast(U32), 0)
+
+        def scale_rows(eng, src, col0, q):
+            eng.dma_start(out=planes[32 * q : 32 * q + 4, col0 : col0 + 512].bitcast(I32), in_=src[0, 4 * q : 4 * q + 4, :].bitcast(I32))
+
+        b_raw = [keep.tile([P, 4, N // 2], F32, name=f"b_raw{h}") for h in range(2)]
+        wb_v = wb.rearrange("(p j) n -> p j n", j=4)
+        nc.sync.dma_start(list_z[:], offs)
+        nc.sync.dma_start(list_u[:], offs2)
+        nc.scalar.dma_start(out=a_raw[:].bitcast(I32), in_=wa_words[0].bitcast(I32))
+        nc.scalar.dma_start(out=x_words[:].bitcast(I32), in_=xt_words[0].rearrange("p n t -> p (n t)").bitcast(I32))
+        for q in range(4):
+            scale_rows(nc.sync, wa_scales, T, q)
+        for q in range(4):
+            scale_rows(nc.sync, xt_scales, 0, q)
+        for h in range(2):
+            nc.sync.dma_start(out=b_raw[h][:], in_=wb_v[:, :, N // 2 * h : N // 2 * (h + 1)])
+        nc.gpsimd.dma_start(out=gains[:], in_=gm.rearrange("(p s) o -> p (s o)", s=S))
+
+
+        a_words = keep.tile([P, 2 * N], U8, name="a_words", align_bytes=64)
+        a_scales = keep.tile([P, N], U8, name="a_scales", align_bytes=64)
+        nc.vector.tensor_copy(out=a_words[:].bitcast(U16).rearrange("p (s m) -> p s m", s=S), in_=a_raw[:].bitcast(U16).rearrange("p (m s) -> p s m", s=S))
+        nc.vector.tensor_copy(out=a_scales[:].rearrange("p (s m) -> p s m", s=S), in_=planes[:, T:].rearrange("p (m s) -> p s m", s=S))
+
+        z = [keep.tile([P, T], F32, name=f"z{s}") for s in range(S)]
+        u = [keep.tile([P, T], F32, name=f"u{s}", tag=f"u{s}", align_bytes=64) for s in range(S)]
+        zg = [None] * S
+        ug = [keep.tile([P, J], F32, name=f"ug{s}") for s in range(S)]
+        b_bf = keep.tile([P, S, P, 4], BF16, name="b_bf", tag="b_bf", align_bytes=64)
+        b_words = keep.tile([P, N], U32, name="b_words", align_bytes=64)
+        b_scales = keep.tile([P, N], U8, name="b_scales", align_bytes=64)
+        out_v = out.rearrange("(p s) j -> p s j", s=S)
+
+        def z_product(s):
+            acc = psum.tile([P, T], F32, name=f"zacc{s}")
+            nc.tensor.matmul_mx(out=acc[:], lhsT=a_words[:, 2 * P * s : 2 * P * (s + 1)].bitcast(FP4X4), lhsT_scale=a_scales[:, P * s : P * (s + 1)],
+                                rhs=x_words[:].bitcast(FP8X4), rhs_scale=planes[:, 0:T], start=True, stop=True)
+            nc.scalar.copy(out=z[s][:], in_=acc[:])
+
+        def u_product(s):
+            acc = psum.tile([P, T], F32, name=f"uacc{s}")
+            nc.tensor.matmul_mx(out=acc[:], lhsT=b_words[:, P * s : P * (s + 1)].bitcast(FP8X4), lhsT_scale=b_scales[:, P * s : P * (s + 1)],
+                                rhs=x_words[:].bitcast(FP8X4), rhs_scale=planes[:, 0:T], start=True, stop=True)
+            nc.scalar.copy(out=u[s][:], in_=acc[:])
+
+        def gather(dst, table, offsets):
+            for h in range(J // H):
+                nc.vector.tensor_copy(dst[:, H * h : H * (h + 1)], table[:].indirect(offsets[:, H // 16 * h : H // 16 * (h + 1)]))
+
+        def z_gather(s, tag):
+            zg[s] = keep.tile([P, J], F32, name=f"zg{s}", tag=tag, align_bytes=64)
+            gather(zg[s], z[s], list_z)
+
+        def cast(h, eng):
+            src = b_raw[h][:].rearrange("p j (m s) -> p m j s", s=S)
+            dst = b_bf[:, :, 64 * h : 64 * (h + 1), :].rearrange("p s m j -> p m j s")
+            if eng == "v":
+                nc.vector.tensor_copy(out=dst, in_=src)
+            elif eng == "s":
+                nc.scalar.copy(out=dst, in_=src)
+            else:
+                nc.gpsimd.tensor_scalar(out=dst, in0=src, scalar1=1.0, scalar2=0.0, op0=ALU.mult, op1=ALU.add)
+
+        def quantise(s):
+            nc.vector.quantize_mx(out=b_words[:, P * s : P * (s + 1)].bitcast(FP8X4), scales=b_scales[:, P * s : P * (s + 1)],
+                                  in_=b_bf[:, s, :, :].rearrange("p m j -> p (m j)"))
+
+        rs = [None] * S
+
+        def recip(s, on_vector):
+            d = keep.tile([P, J], F32, name=f"d{s}")
+            if on_vector:
+                nc.vector.tensor_scalar(out=d[:], in0=ug[s][:], scalar1=0.0, scalar2=None, op0=ALU.max)
+            else:
+                nc.scalar.activation(d[:], ug[s][:], ACT.Relu)
+            root = keep.tile([P, J], F32, name=f"root{s}")
+            nc.scalar.activation(root[:], d[:], ACT.Abs_reciprocal_sqrt, bias=1.0)
+            rs[s] = keep.tile([P, J], F32, name=f"rs{s}")
+            nc.scalar.activation(rs[s][:], root[:], ACT.Square)
+
+        def finish(s, tag):
+            y = keep.tile([P, J], F32, name=f"y{s}", tag=tag)
+            nc.vector.scalar_tensor_tensor(out=y[:], in0=zg[s][:], scalar=gains[:, s : s + 1], in1=rs[s][:], op0=ALU.mult, op1=ALU.mult)
+            nc.sync.dma_start(out=out_v[:, s, :], in_=y[:])
+
+        for s in range(3):
+            z_product(s)
+            z_gather(s, f"zg{s}")
+        for h in range(2):
+            cast(h, "s")
+        z_product(3)
+        for s in range(S):
+            quantise(s)
+        z_gather(3, "b_bf")
+        for s in range(S):
+            u_product(s)
+        for s in range(S):
+            gather(ug[s], u[s], list_u)
+            recip(s, s >= 2)
+        for s in range(S):
+            finish(s, f"y{s}")

@@ -27,54 +27,65 @@ def tile_list_head_divided_by_own_list_kernel(tc, xt_words, xt_scales, wa_words,
 
         list_z = keep.tile([P, J // 16], U16, name="list_z")
         list_u = keep.tile([P, J // 16], U16, name="list_u")
-        planes = keep.tile([P, T + N], U8, name="planes", align_bytes=64)
+        x_scales = keep.tile([P, T], U8, name="x_scales", align_bytes=64)
+        a_scales_raw = keep.tile([P, N], U8, name="a_scales_raw", tag="a_scales_raw", align_bytes=64)
         x_words = keep.tile([P, T], U32, name="x_words", align_bytes=64)
-        a_raw = keep.tile([P, 2 * N], U8, name="a_raw", align_bytes=64)
+        nc.gpsimd.memset(x_scales[:].bitcast(U32), 0)
+        nc.gpsimd.memset(a_scales_raw[:].bitcast(U32), 0)
+        warm = keep.tile([P, 1], F32, name="warm")
+        warmed = keep.tile([P, 1], F32, name="warmed")
+        nc.vector.memset(warm[:], 1.0)
+
+        nc.scalar.activation(warmed[:], warm[:], ACT.Abs_reciprocal_sqrt)
+        a_raw = keep.tile([P, 2 * N], U8, name="a_raw", tag="a_raw", align_bytes=64)
+
         gains = keep.tile([P, S], F32, name="gains")
-        nc.gpsimd.memset(planes[:].bitcast(U32), 0)
 
-        def scale_rows(eng, src, col0, q):
-            eng.dma_start(out=planes[32 * q : 32 * q + 4, col0 : col0 + 512].bitcast(I32), in_=src[0, 4 * q : 4 * q + 4, :].bitcast(I32))
+        def scale_rows(eng, src, plane, q):
+            eng.dma_start(out=plane[32 * q : 32 * q + 4, :].bitcast(I32), in_=src[0, 4 * q : 4 * q + 4, :].bitcast(I32))
 
-        b_raw = [keep.tile([P, 4, N // 2], F32, name=f"b_raw{h}") for h in range(2)]
+        b_raw = keep.tile([P, 4, N], F32, name="b_raw")
         wb_v = wb.rearrange("(p j) n -> p j n", j=4)
-        nc.sync.dma_start(list_z[:], offs)
         nc.sync.dma_start(list_u[:], offs2)
-        nc.scalar.dma_start(out=a_raw[:].bitcast(I32), in_=wa_words[0].bitcast(I32))
-        nc.scalar.dma_start(out=x_words[:].bitcast(I32), in_=xt_words[0].rearrange("p n t -> p (n t)").bitcast(I32))
+        nc.sync.dma_start(list_z[:], offs)
+        nc.sync.dma_start(out=gains[:], in_=gm.rearrange("(p s) o -> p (s o)", s=S))
+        nc.sync.dma_start(out=a_raw[:].bitcast(I32), in_=wa_words[0].bitcast(I32))
+        nc.sync.dma_start(out=b_raw[:], in_=wb_v)
+        nc.sync.dma_start(out=x_words[:].bitcast(I32), in_=xt_words[0].rearrange("p n t -> p (n t)").bitcast(I32))
         for q in range(4):
-            scale_rows(nc.sync, wa_scales, T, q)
-        for q in range(4):
-            scale_rows(nc.sync, xt_scales, 0, q)
-        for h in range(2):
-            nc.sync.dma_start(out=b_raw[h][:], in_=wb_v[:, :, N // 2 * h : N // 2 * (h + 1)])
-        nc.gpsimd.dma_start(out=gains[:], in_=gm.rearrange("(p s) o -> p (s o)", s=S))
+            scale_rows(nc.sync, xt_scales, x_scales, q)
+        for q in range(2):
+            scale_rows(nc.sync, wa_scales, a_scales_raw, q)
+        for q in range(2, 4):
+            scale_rows(nc.gpsimd, wa_scales, a_scales_raw, q)
 
 
         a_words = keep.tile([P, 2 * N], U8, name="a_words", align_bytes=64)
         a_scales = keep.tile([P, N], U8, name="a_scales", align_bytes=64)
-        nc.vector.tensor_copy(out=a_words[:].bitcast(U16).rearrange("p (s m) -> p s m", s=S), in_=a_raw[:].bitcast(U16).rearrange("p (m s) -> p s m", s=S))
-        nc.vector.tensor_copy(out=a_scales[:].rearrange("p (s m) -> p s m", s=S), in_=planes[:, T:].rearrange("p (m s) -> p s m", s=S))
 
-        z = [keep.tile([P, T], F32, name=f"z{s}") for s in range(S)]
+        def deal_a():
+            nc.vector.tensor_copy(out=a_words[:].bitcast(U16).rearrange("p (s m) -> p s m", s=S), in_=a_raw[:].bitcast(U16).rearrange("p (m s) -> p s m", s=S))
+            nc.vector.tensor_copy(out=a_scales[:].rearrange("p (s m) -> p s m", s=S), in_=a_scales_raw[:].rearrange("p (m s) -> p s m", s=S))
+
+        z = [keep.tile([P, T], F32, name=f"z{s}", tag=f"z{s}") for s in range(S)]
         u = [keep.tile([P, T], F32, name=f"u{s}", tag=f"u{s}", align_bytes=64) for s in range(S)]
         zg = [None] * S
-        ug = [keep.tile([P, J], F32, name=f"ug{s}") for s in range(S)]
+        ug = [None] * S
         b_bf = keep.tile([P, S, P, 4], BF16, name="b_bf", tag="b_bf", align_bytes=64)
         b_words = keep.tile([P, N], U32, name="b_words", align_bytes=64)
         b_scales = keep.tile([P, N], U8, name="b_scales", align_bytes=64)
         out_v = out.rearrange("(p s) j -> p s j", s=S)
 
-        def z_product(s):
-            acc = psum.tile([P, T], F32, name=f"zacc{s}")
+        def z_product(s, tag):
+            acc = psum.tile([P, T], F32, name=f"zacc{s}", tag=tag)
             nc.tensor.matmul_mx(out=acc[:], lhsT=a_words[:, 2 * P * s : 2 * P * (s + 1)].bitcast(FP4X4), lhsT_scale=a_scales[:, P * s : P * (s + 1)],
-                                rhs=x_words[:].bitcast(FP8X4), rhs_scale=planes[:, 0:T], start=True, stop=True)
+                                rhs=x_words[:].bitcast(FP8X4), rhs_scale=x_scales[:], start=True, stop=True)
             nc.scalar.copy(out=z[s][:], in_=acc[:])
 
         def u_product(s):
-            acc = psum.tile([P, T], F32, name=f"uacc{s}")
+            acc = psum.tile([P, T], F32, name=f"uacc{s}", tag=f"uacc{s}")
             nc.tensor.matmul_mx(out=acc[:], lhsT=b_words[:, P * s : P * (s + 1)].bitcast(FP8X4), lhsT_scale=b_scales[:, P * s : P * (s + 1)],
-                                rhs=x_words[:].bitcast(FP8X4), rhs_scale=planes[:, 0:T], start=True, stop=True)
+                                rhs=x_words[:].bitcast(FP8X4), rhs_scale=x_scales[:], start=True, stop=True)
             nc.scalar.copy(out=u[s][:], in_=acc[:])
 
         def gather(dst, table, offsets):
@@ -85,9 +96,13 @@ def tile_list_head_divided_by_own_list_kernel(tc, xt_words, xt_scales, wa_words,
             zg[s] = keep.tile([P, J], F32, name=f"zg{s}", tag=tag, align_bytes=64)
             gather(zg[s], z[s], list_z)
 
-        def cast(h, eng):
-            src = b_raw[h][:].rearrange("p j (m s) -> p m j s", s=S)
-            dst = b_bf[:, :, 64 * h : 64 * (h + 1), :].rearrange("p s m j -> p m j s")
+        def u_gather(s, tag):
+            ug[s] = keep.tile([P, J], F32, name=f"ug{s}", tag=tag, align_bytes=64)
+            gather(ug[s], u[s], list_u)
+
+        def cast(m0, m1, eng):
+            src = b_raw[:, :, S * m0 : S * m1].rearrange("p j (m s) -> p m j s", s=S)
+            dst = b_bf[:, :, m0:m1, :].rearrange("p s m j -> p m j s")
             if eng == "v":
                 nc.vector.tensor_copy(out=dst, in_=src)
             elif eng == "s":
@@ -101,35 +116,58 @@ def tile_list_head_divided_by_own_list_kernel(tc, xt_words, xt_scales, wa_words,
 
         rs = [None] * S
 
-        def recip(s, on_vector):
-            d = keep.tile([P, J], F32, name=f"d{s}")
-            if on_vector:
-                nc.vector.tensor_scalar(out=d[:], in0=ug[s][:], scalar1=0.0, scalar2=None, op0=ALU.max)
-            else:
-                nc.scalar.activation(d[:], ug[s][:], ACT.Relu)
-            root = keep.tile([P, J], F32, name=f"root{s}")
-            nc.scalar.activation(root[:], d[:], ACT.Abs_reciprocal_sqrt, bias=1.0)
+        d = [None] * S
+        root = [None] * S
+
+        def positive(s):
+            d[s] = keep.tile([P, J], F32, name=f"d{s}")
+            nc.gpsimd.tensor_scalar(out=d[s][:], in0=ug[s][:], scalar1=0.0, scalar2=1.0, op0=ALU.max, op1=ALU.add)
+
+        def inv_root(s):
+            root[s] = keep.tile([P, J], F32, name=f"root{s}")
+            nc.scalar.activation(root[s][:], d[s][:], ACT.Abs_reciprocal_sqrt)
+
+        def square(s):
             rs[s] = keep.tile([P, J], F32, name=f"rs{s}")
-            nc.scalar.activation(rs[s][:], root[:], ACT.Square)
+            nc.scalar.activation(rs[s][:], root[s][:], ACT.Square)
+
+        def finish_g(s):
+            scaled = keep.tile([P, J], F32, name=f"scaled{s}")
+            nc.gpsimd.tensor_scalar(out=scaled[:], in0=rs[s][:], scalar1=gains[:, s : s + 1], scalar2=0.0, op0=ALU.mult, op1=ALU.add)
+            y = keep.tile([P, J], F32, name=f"y{s}")
+            nc.gpsimd.tensor_tensor(out=y[:], in0=zg[s][:], in1=scaled[:], op=ALU.mult)
+            nc.sync.dma_start(out=out_v[:, s, :], in_=y[:])
 
         def finish(s, tag):
             y = keep.tile([P, J], F32, name=f"y{s}", tag=tag)
             nc.vector.scalar_tensor_tensor(out=y[:], in0=zg[s][:], scalar=gains[:, s : s + 1], in1=rs[s][:], op0=ALU.mult, op1=ALU.mult)
             nc.sync.dma_start(out=out_v[:, s, :], in_=y[:])
 
-        for s in range(3):
-            z_product(s)
-            z_gather(s, f"zg{s}")
-        for h in range(2):
-            cast(h, "s")
-        z_product(3)
+        cast(0, 84, "v")
+        cast(84, 128, "s")
         for s in range(S):
             quantise(s)
-        z_gather(3, "b_bf")
         for s in range(S):
             u_product(s)
+        deal_a()
+        u_gather(0, "a_scales_raw")
+        for s in range(1, S):
+            u_gather(s, f"ug{s}")
         for s in range(S):
-            gather(ug[s], u[s], list_u)
-            recip(s, s >= 2)
+            positive(s)
         for s in range(S):
-            finish(s, f"y{s}")
+            inv_root(s)
+            z_product(s, f"zacc{s}")
+            z_gather(s, f"zg{s}")
+            if s == 2:
+                z_product(3, "zacc3")
+                z_gather(3, "zg3")
+            square(s)
+            if s < 2:
+                finish_g(s)
+            if s == 2:
+                break
+        inv_root(3)
+        square(3)
+        finish(2, "y2")
+        finish(3, "y3")

@@ -44,13 +44,14 @@ def tile_list_head_divided_by_own_list_kernel(tc, xt_words, xt_scales, wa_words,
         def scale_rows(eng, src, plane, q):
             eng.dma_start(out=plane[32 * q : 32 * q + 4, :].bitcast(I32), in_=src[0, 4 * q : 4 * q + 4, :].bitcast(I32))
 
-        b_raw = keep.tile([P, 4, N], F32, name="b_raw")
+        b_raw = [keep.tile([P, 4, N // 2], F32, name=f"b_raw{h}") for h in range(2)]
         wb_v = wb.rearrange("(p j) n -> p j n", j=4)
         nc.sync.dma_start(list_u[:], offs2)
         nc.sync.dma_start(list_z[:], offs)
         nc.sync.dma_start(out=gains[:], in_=gm.rearrange("(p s) o -> p (s o)", s=S))
         nc.sync.dma_start(out=a_raw[:].bitcast(I32), in_=wa_words[0].bitcast(I32))
-        nc.sync.dma_start(out=b_raw[:], in_=wb_v)
+        for h in range(2):
+            nc.sync.dma_start(out=b_raw[h][:], in_=wb_v[:, :, N // 2 * h : N // 2 * (h + 1)])
         nc.sync.dma_start(out=x_words[:].bitcast(I32), in_=xt_words[0].rearrange("p n t -> p (n t)").bitcast(I32))
         for q in range(4):
             scale_rows(nc.sync, xt_scales, x_scales, q)
@@ -96,12 +97,13 @@ def tile_list_head_divided_by_own_list_kernel(tc, xt_words, xt_scales, wa_words,
             zg[s] = keep.tile([P, J], F32, name=f"zg{s}", tag=tag, align_bytes=64)
             gather(zg[s], z[s], list_z)
 
-        def u_gather(s, tag):
-            ug[s] = keep.tile([P, J], F32, name=f"ug{s}", tag=tag, align_bytes=64)
+
+        def u_gather(s):
+            ug[s] = ug01[:, J * s : J * (s + 1)] if s < 2 else keep.tile([P, J], F32, name=f"ug{s}")
             gather(ug[s], u[s], list_u)
 
         def cast(m0, m1, eng):
-            src = b_raw[:, :, S * m0 : S * m1].rearrange("p j (m s) -> p m j s", s=S)
+            src = b_raw[m0 // 64][:, :, S * (m0 % 64) : S * ((m1 - 1) % 64 + 1)].rearrange("p j (m s) -> p m j s", s=S)
             dst = b_bf[:, :, m0:m1, :].rearrange("p s m j -> p m j s")
             if eng == "v":
                 nc.vector.tensor_copy(out=dst, in_=src)
@@ -121,52 +123,62 @@ def tile_list_head_divided_by_own_list_kernel(tc, xt_words, xt_scales, wa_words,
 
         def positive(s):
             d[s] = keep.tile([P, J], F32, name=f"d{s}")
-            nc.gpsimd.tensor_scalar(out=d[s][:], in0=ug[s][:], scalar1=0.0, scalar2=1.0, op0=ALU.max, op1=ALU.add)
+            nc.scalar.activation(d[s][:], ug[s][:], ACT.Relu)
 
         def inv_root(s):
             root[s] = keep.tile([P, J], F32, name=f"root{s}")
-            nc.scalar.activation(root[s][:], d[s][:], ACT.Abs_reciprocal_sqrt)
+            nc.scalar.activation(root[s][:], d[s][:], ACT.Abs_reciprocal_sqrt, bias=1.0)
 
         def square(s):
             rs[s] = keep.tile([P, J], F32, name=f"rs{s}")
             nc.scalar.activation(rs[s][:], root[s][:], ACT.Square)
 
-        def finish_g(s):
-            scaled = keep.tile([P, J], F32, name=f"scaled{s}")
-            nc.gpsimd.tensor_scalar(out=scaled[:], in0=rs[s][:], scalar1=gains[:, s : s + 1], scalar2=0.0, op0=ALU.mult, op1=ALU.add)
-            y = keep.tile([P, J], F32, name=f"y{s}")
-            nc.gpsimd.tensor_tensor(out=y[:], in0=zg[s][:], in1=scaled[:], op=ALU.mult)
-            nc.sync.dma_start(out=out_v[:, s, :], in_=y[:])
+        def positive01():
+            d[0] = keep.tile([P, 2 * J], F32, name="d01")
+            nc.scalar.activation(d[0][:], ug01[:], ACT.Relu)
+
+        def inv_root01():
+            root[0] = keep.tile([P, 2 * J], F32, name="root01")
+            nc.scalar.activation(root[0][:], d[0][:], ACT.Abs_reciprocal_sqrt, bias=1.0)
+
+        def square01():
+            rs01 = keep.tile([P, 2 * J], F32, name="rs01")
+            nc.scalar.activation(rs01[:], root[0][:], ACT.Square)
+            rs[0] = rs01[:, :J]
+            rs[1] = rs01[:, J:]
 
         def finish(s, tag):
             y = keep.tile([P, J], F32, name=f"y{s}", tag=tag)
             nc.vector.scalar_tensor_tensor(out=y[:], in0=zg[s][:], scalar=gains[:, s : s + 1], in1=rs[s][:], op0=ALU.mult, op1=ALU.mult)
             nc.sync.dma_start(out=out_v[:, s, :], in_=y[:])
 
-        cast(0, 84, "v")
-        cast(84, 128, "s")
+        cast(0, 64, "v")
+        cast(64, 108, "v")
+        cast(108, 128, "s")
         for s in range(S):
             quantise(s)
+        deal_a()
+        ug01 = keep.tile([P, 2 * J], F32, name="ug01", tag="a_scales_raw", align_bytes=64)
         for s in range(S):
             u_product(s)
-        deal_a()
-        u_gather(0, "a_scales_raw")
-        for s in range(1, S):
-            u_gather(s, f"ug{s}")
-        for s in range(S):
-            positive(s)
-        for s in range(S):
-            inv_root(s)
-            z_product(s, f"zacc{s}")
-            z_gather(s, f"zg{s}")
-            if s == 2:
-                z_product(3, "zacc3")
-                z_gather(3, "zg3")
-            square(s)
-            if s < 2:
-                finish_g(s)
-            if s == 2:
-                break
+            u_gather(s)
+        z_product(0, "uacc0")
+        z_gather(0, "zg0")
+        positive01()
+        z_product(1, "uacc1")
+        z_gather(1, "zg1")
+        inv_root01()
+        positive(2)
+        square01()
+        z_product(2, "uacc2")
+        z_gather(2, "zg2")
+        finish(0, "y0")
+        finish(1, "y1")
+        inv_root(2)
+        positive(3)
+        z_product(3, "uacc3")
+        z_gather(3, "zg3")
+        square(2)
         inv_root(3)
         square(3)
         finish(2, "y2")

@@ -16,6 +16,7 @@ ACT = mybir.ActivationFunctionType
 ALU = mybir.AluOpType
 P = 128
 S = 4
+Q = 64
 H = 256
 
 
@@ -35,151 +36,119 @@ def tile_list_head_divided_by_own_list_kernel(tc, xt_words, xt_scales, wa_words,
         warm = keep.tile([P, 1], F32, name="warm")
         warmed = keep.tile([P, 1], F32, name="warmed")
         nc.vector.memset(warm[:], 1.0)
-
         nc.scalar.activation(warmed[:], warm[:], ACT.Abs_reciprocal_sqrt)
-        a_raw = keep.tile([P, 2 * N], U8, name="a_raw", tag="a_raw", align_bytes=64)
+        a_raw = keep.tile([P, 2 * N], U8, name="a_raw", align_bytes=64)
+        gains = keep.tile([P, 2 * S], F32, name="gains")
 
-        gains = keep.tile([P, S], F32, name="gains")
-
-        def scale_rows(eng, src, plane, q):
-            eng.dma_start(out=plane[32 * q : 32 * q + 4, :].bitcast(I32), in_=src[0, 4 * q : 4 * q + 4, :].bitcast(I32))
+        def scale_rows(eng, src, plane, quad):
+            eng.dma_start(out=plane[32 * quad : 32 * quad + 4, :].bitcast(I32), in_=src[0, 4 * quad : 4 * quad + 4, :].bitcast(I32))
 
         b_raw = [keep.tile([P, 4, N // 2], F32, name=f"b_raw{h}") for h in range(2)]
         wb_v = wb.rearrange("(p j) n -> p j n", j=4)
         nc.sync.dma_start(list_u[:], offs2)
         nc.sync.dma_start(list_z[:], offs)
-        nc.sync.dma_start(out=gains[:], in_=gm.rearrange("(p s) o -> p (s o)", s=S))
+        gm_v = gm.rearrange("(q e) o -> q (e o)", e=2 * S)
+        for b in range(2):
+            nc.sync.dma_start(out=gains[b:P:2, 0 : 2 * S - 1], in_=gm_v[:, b : b + 2 * S - 1])
         nc.sync.dma_start(out=a_raw[:].bitcast(I32), in_=wa_words[0].bitcast(I32))
         for h in range(2):
             nc.sync.dma_start(out=b_raw[h][:], in_=wb_v[:, :, N // 2 * h : N // 2 * (h + 1)])
         nc.sync.dma_start(out=x_words[:].bitcast(I32), in_=xt_words[0].rearrange("p n t -> p (n t)").bitcast(I32))
-        for q in range(4):
-            scale_rows(nc.sync, xt_scales, x_scales, q)
-        for q in range(2):
-            scale_rows(nc.sync, wa_scales, a_scales_raw, q)
-        for q in range(2, 4):
-            scale_rows(nc.gpsimd, wa_scales, a_scales_raw, q)
+        for quad in range(4):
+            scale_rows(nc.sync, xt_scales, x_scales, quad)
+        for quad in range(4):
+            scale_rows(nc.sync if quad < 2 else nc.gpsimd, wa_scales, a_scales_raw, quad)
 
-
-        a_words = keep.tile([P, 2 * N], U8, name="a_words", align_bytes=64)
         a_scales = keep.tile([P, N], U8, name="a_scales", align_bytes=64)
-
-        def deal_a():
-            nc.vector.tensor_copy(out=a_words[:].bitcast(U16).rearrange("p (s m) -> p s m", s=S), in_=a_raw[:].bitcast(U16).rearrange("p (m s) -> p s m", s=S))
-            nc.vector.tensor_copy(out=a_scales[:].rearrange("p (s m) -> p s m", s=S), in_=a_scales_raw[:].rearrange("p (m s) -> p s m", s=S))
-
-        z = [keep.tile([P, T], F32, name=f"z{s}", tag=f"z{s}") for s in range(S)]
+        a_words = keep.tile([P, 2 * N], U8, name="a_words", align_bytes=64)
+        z = [keep.tile([P, T], F32, name=f"z{s}") for s in range(S)]
         u = [keep.tile([P, T], F32, name=f"u{s}", tag=f"u{s}", align_bytes=64) for s in range(S)]
-        zg = [None] * S
-        ug = [None] * S
-        b_bf = keep.tile([P, S, P, 4], BF16, name="b_bf", tag="b_bf", align_bytes=64)
+        b_bf = keep.tile([P, S, Q, 2, 4], BF16, name="b_bf", align_bytes=64)
         b_words = keep.tile([P, N], U32, name="b_words", align_bytes=64)
         b_scales = keep.tile([P, N], U8, name="b_scales", align_bytes=64)
-        out_v = out.rearrange("(p s) j -> p s j", s=S)
+        out_v = out.rearrange("(q s b) j -> b q s j", s=S, b=2)
+        zg, ug, d, root, rs = ([None] * S for i in range(5))
 
-        def z_product(s, tag):
-            acc = psum.tile([P, T], F32, name=f"zacc{s}", tag=tag)
+        def deal_a():
+            nc.vector.tensor_copy(out=a_words[:].bitcast(I32).rearrange("p (s q) -> p s q", s=S), in_=a_raw[:].bitcast(I32).rearrange("p (q s) -> p s q", s=S))
+            nc.vector.tensor_copy(out=a_scales[:].bitcast(U16).rearrange("p (s q) -> p s q", s=S), in_=a_scales_raw[:].bitcast(U16).rearrange("p (q s) -> p s q", s=S))
+
+        def z_product(s):
+            acc = psum.tile([P, T], F32, name=f"zacc{s}", tag=f"acc{s}")
             nc.tensor.matmul_mx(out=acc[:], lhsT=a_words[:, 2 * P * s : 2 * P * (s + 1)].bitcast(FP4X4), lhsT_scale=a_scales[:, P * s : P * (s + 1)],
                                 rhs=x_words[:].bitcast(FP8X4), rhs_scale=x_scales[:], start=True, stop=True)
             nc.scalar.copy(out=z[s][:], in_=acc[:])
 
-        def u_product(s):
-            acc = psum.tile([P, T], F32, name=f"uacc{s}", tag=f"uacc{s}")
+        def u_product(s, cols, tag, copy):
+            acc = psum.tile([P, cols.stop - cols.start], F32, name=f"uacc{s}_{cols.start}", tag=tag)
             nc.tensor.matmul_mx(out=acc[:], lhsT=b_words[:, P * s : P * (s + 1)].bitcast(FP8X4), lhsT_scale=b_scales[:, P * s : P * (s + 1)],
-                                rhs=x_words[:].bitcast(FP8X4), rhs_scale=x_scales[:], start=True, stop=True)
-            nc.scalar.copy(out=u[s][:], in_=acc[:])
+                                rhs=x_words[:, cols].bitcast(FP8X4), rhs_scale=x_scales[:, cols], start=True, stop=True)
+            copy(out=u[s][:, cols], in_=acc[:])
 
         def gather(dst, table, offsets):
             for h in range(J // H):
                 nc.vector.tensor_copy(dst[:, H * h : H * (h + 1)], table[:].indirect(offsets[:, H // 16 * h : H // 16 * (h + 1)]))
 
-        def z_gather(s, tag):
-            zg[s] = keep.tile([P, J], F32, name=f"zg{s}", tag=tag, align_bytes=64)
+        def z_gather(s):
+            zg[s] = keep.tile([P, J], F32, name=f"zg{s}")
             gather(zg[s], z[s], list_z)
 
-
-        def u_gather(s):
-            ug[s] = ug01[:, J * s : J * (s + 1)] if s < 2 else keep.tile([P, J], F32, name=f"ug{s}")
-            gather(ug[s], u[s], list_u)
-
-        def cast(m0, m1, eng):
-            src = b_raw[m0 // 64][:, :, S * (m0 % 64) : S * ((m1 - 1) % 64 + 1)].rearrange("p j (m s) -> p m j s", s=S)
-            dst = b_bf[:, :, m0:m1, :].rearrange("p s m j -> p m j s")
-            if eng == "v":
-                nc.vector.tensor_copy(out=dst, in_=src)
-            elif eng == "s":
-                nc.scalar.copy(out=dst, in_=src)
-            else:
-                nc.gpsimd.tensor_scalar(out=dst, in0=src, scalar1=1.0, scalar2=0.0, op0=ALU.mult, op1=ALU.add)
+        def cast(q0, q1, copy):
+            half = q0 // 32
+            src = b_raw[half][:, :, 8 * (q0 - 32 * half) : 8 * (q1 - 32 * half)].rearrange("p j (q s b) -> p q s b j", s=S, b=2)
+            copy(out=b_bf[:, :, q0:q1, :, :].rearrange("p s q b j -> p q s b j"), in_=src)
 
         def quantise(s):
             nc.vector.quantize_mx(out=b_words[:, P * s : P * (s + 1)].bitcast(FP8X4), scales=b_scales[:, P * s : P * (s + 1)],
-                                  in_=b_bf[:, s, :, :].rearrange("p m j -> p (m j)"))
+                                  in_=b_bf[:, s, :, :, :].rearrange("p q b j -> p (q b j)"))
 
-        rs = [None] * S
+        def positive(s, src, width):
+            d[s] = keep.tile([P, width], F32, name=f"d{s}")
+            nc.scalar.activation(d[s][:], src, ACT.Relu)
 
-        d = [None] * S
-        root = [None] * S
-
-        def positive(s):
-            d[s] = keep.tile([P, J], F32, name=f"d{s}")
-            nc.scalar.activation(d[s][:], ug[s][:], ACT.Relu)
-
-        def inv_root(s):
-            root[s] = keep.tile([P, J], F32, name=f"root{s}")
+        def inv_root(s, width):
+            root[s] = keep.tile([P, width], F32, name=f"root{s}")
             nc.scalar.activation(root[s][:], d[s][:], ACT.Abs_reciprocal_sqrt, bias=1.0)
 
-        def square(s):
-            rs[s] = keep.tile([P, J], F32, name=f"rs{s}")
+        def square(s, width):
+            rs[s] = keep.tile([P, width], F32, name=f"rs{s}")
             nc.scalar.activation(rs[s][:], root[s][:], ACT.Square)
 
-        def positive01():
-            d[0] = keep.tile([P, 2 * J], F32, name="d01")
-            nc.scalar.activation(d[0][:], ug01[:], ACT.Relu)
+        def finish(s, r):
+            y = keep.tile([P, J], F32, name=f"y{s}")
+            nc.vector.scalar_tensor_tensor(out=y[:], in0=zg[s][:], scalar=gains[:, 2 * s : 2 * s + 1], in1=r, op0=ALU.mult, op1=ALU.mult)
+            for b in range(2):
+                nc.sync.dma_start(out=out_v[b][:, s, :], in_=y[b:P:2, :])
 
-        def inv_root01():
-            root[0] = keep.tile([P, 2 * J], F32, name="root01")
-            nc.scalar.activation(root[0][:], d[0][:], ACT.Abs_reciprocal_sqrt, bias=1.0)
-
-        def square01():
-            rs01 = keep.tile([P, 2 * J], F32, name="rs01")
-            nc.scalar.activation(rs01[:], root[0][:], ACT.Square)
-            rs[0] = rs01[:, :J]
-            rs[1] = rs01[:, J:]
-
-        def finish(s, tag):
-            y = keep.tile([P, J], F32, name=f"y{s}", tag=tag)
-            nc.vector.scalar_tensor_tensor(out=y[:], in0=zg[s][:], scalar=gains[:, s : s + 1], in1=rs[s][:], op0=ALU.mult, op1=ALU.mult)
-            nc.sync.dma_start(out=out_v[:, s, :], in_=y[:])
-
-        cast(0, 64, "v")
-        cast(64, 108, "v")
-        cast(108, 128, "s")
+        cast(0, 32, nc.vector.tensor_copy)
+        cast(32, 54, nc.vector.tensor_copy)
+        cast(54, 64, nc.scalar.copy)
         for s in range(S):
             quantise(s)
         deal_a()
         ug01 = keep.tile([P, 2 * J], F32, name="ug01", tag="a_scales_raw", align_bytes=64)
         for s in range(S):
-            u_product(s)
-            u_gather(s)
-        z_product(0, "uacc0")
-        z_gather(0, "zg0")
-        positive01()
-        z_product(1, "uacc1")
-        z_gather(1, "zg1")
-        inv_root01()
-        positive(2)
-        square01()
-        z_product(2, "uacc2")
-        z_gather(2, "zg2")
-        finish(0, "y0")
-        finish(1, "y1")
-        inv_root(2)
-        positive(3)
-        z_product(3, "uacc3")
-        z_gather(3, "zg3")
-        square(2)
-        inv_root(3)
-        square(3)
-        finish(2, "y2")
-        finish(3, "y3")
+            u_product(s, slice(0, T), f"acc{s}", nc.scalar.copy)
+            ug[s] = ug01[:, J * s : J * (s + 1)] if s < 2 else keep.tile([P, J], F32, name=f"ug{s}")
+            gather(ug[s], u[s], list_u)
+        z_product(0)
+        z_gather(0)
+        positive(0, ug01[:], 2 * J)
+        z_product(1)
+        z_gather(1)
+        inv_root(0, 2 * J)
+        positive(2, ug[2][:], J)
+        square(0, 2 * J)
+        z_product(2)
+        z_gather(2)
+        finish(0, rs[0][:, :J])
+        finish(1, rs[0][:, J:])
+        inv_root(2, J)
+        positive(3, ug[3][:], J)
+        z_product(3)
+        z_gather(3)
+        square(2, J)
+        inv_root(3, J)
+        square(3, J)
+        finish(2, rs[2][:])
+        finish(3, rs[3][:])

@@ -4,6 +4,7 @@ import concourse.mybir as mybir
 
 K, T, J, N = 512, 512, 512, 512
 FLOPS = 2 * 2 * K * N * T
+
 F32 = mybir.dt.float32
 BF16 = mybir.dt.bfloat16
 I32 = mybir.dt.int32
@@ -14,10 +15,14 @@ FP8X4 = mybir.dt.float8_e4m3fn_x4
 FP4X4 = mybir.dt.float4_e2m1fn_x4
 ACT = mybir.ActivationFunctionType
 ALU = mybir.AluOpType
+
 P = 128
-S = 4
-Q = 64
-H = 256
+PACK = 4
+SLICES = N // P
+PAIRS = P // 2
+RUN = 2 * SLICES
+QUADRANTS = 4
+VECTOR_ROUNDS_UP_TO = 54
 
 
 def tile_list_head_divided_by_own_list_kernel(tc, xt_words, xt_scales, wa_words, wa_scales, wb, gm, offs, offs2, out):
@@ -33,122 +38,117 @@ def tile_list_head_divided_by_own_list_kernel(tc, xt_words, xt_scales, wa_words,
         x_words = keep.tile([P, T], U32, name="x_words", align_bytes=64)
         nc.gpsimd.memset(x_scales[:].bitcast(U32), 0)
         nc.gpsimd.memset(a_scales_raw[:].bitcast(U32), 0)
+
         warm = keep.tile([P, 1], F32, name="warm")
         warmed = keep.tile([P, 1], F32, name="warmed")
         nc.vector.memset(warm[:], 1.0)
         nc.scalar.activation(warmed[:], warm[:], ACT.Abs_reciprocal_sqrt)
+
         a_raw = keep.tile([P, 2 * N], U8, name="a_raw", align_bytes=64)
-        gains = keep.tile([P, 2 * S], F32, name="gains")
+        gains = keep.tile([P, RUN], F32, name="gains")
+        b_raw = [keep.tile([P, PACK, N // 2], F32, name=f"b_raw{half}") for half in range(2)]
 
-        def scale_rows(eng, src, plane, quad):
-            eng.dma_start(out=plane[32 * quad : 32 * quad + 4, :].bitcast(I32), in_=src[0, 4 * quad : 4 * quad + 4, :].bitcast(I32))
+        def load_scale_rows(queue, src, dst, quad):
+            queue.dma_start(out=dst[32 * quad : 32 * quad + 4, :].bitcast(I32), in_=src[0, 4 * quad : 4 * quad + 4, :].bitcast(I32))
 
-        b_raw = [keep.tile([P, 4, N // 2], F32, name=f"b_raw{h}") for h in range(2)]
-        wb_v = wb.rearrange("(p j) n -> p j n", j=4)
         nc.sync.dma_start(list_u[:], offs2)
         nc.sync.dma_start(list_z[:], offs)
-        gm_v = gm.rearrange("(q e) o -> q (e o)", e=2 * S)
+        gm_runs = gm.rearrange("(q e) o -> q (e o)", e=RUN)
         for b in range(2):
-            nc.sync.dma_start(out=gains[b:P:2, 0 : 2 * S - 1], in_=gm_v[:, b : b + 2 * S - 1])
+            nc.sync.dma_start(out=gains[b:P:2, 0 : RUN - 1], in_=gm_runs[:, b : b + RUN - 1])
         nc.sync.dma_start(out=a_raw[:].bitcast(I32), in_=wa_words[0].bitcast(I32))
-        for h in range(2):
-            nc.sync.dma_start(out=b_raw[h][:], in_=wb_v[:, :, N // 2 * h : N // 2 * (h + 1)])
-        nc.sync.dma_start(out=x_words[:].bitcast(I32), in_=xt_words[0].rearrange("p n t -> p (n t)").bitcast(I32))
-        for quad in range(4):
-            scale_rows(nc.sync, xt_scales, x_scales, quad)
-        for quad in range(4):
-            scale_rows(nc.sync if quad < 2 else nc.gpsimd, wa_scales, a_scales_raw, quad)
+        wb_rows = wb.rearrange("(p t) n -> p t n", t=PACK)
+        for half in range(2):
+            nc.sync.dma_start(out=b_raw[half][:], in_=wb_rows[:, :, N // 2 * half : N // 2 * (half + 1)])
+        nc.sync.dma_start(out=x_words[:].bitcast(I32), in_=xt_words[0].rearrange("p c t -> p (c t)").bitcast(I32))
+        for quad in range(QUADRANTS):
+            load_scale_rows(nc.sync, xt_scales, x_scales, quad)
+        for quad in range(QUADRANTS):
+            load_scale_rows(nc.sync if quad < QUADRANTS // 2 else nc.gpsimd, wa_scales, a_scales_raw, quad)
 
         a_scales = keep.tile([P, N], U8, name="a_scales", align_bytes=64)
         a_words = keep.tile([P, 2 * N], U8, name="a_words", align_bytes=64)
-        z = [keep.tile([P, T], F32, name=f"z{s}") for s in range(S)]
-        u = [keep.tile([P, T], F32, name=f"u{s}", tag=f"u{s}", align_bytes=64) for s in range(S)]
-        b_bf = keep.tile([P, S, Q, 2, 4], BF16, name="b_bf", align_bytes=64)
+        table = [keep.tile([P, 2 * T], F32, name=f"table{s}") for s in range(SLICES)]
+        for s in range(SLICES):
+            nc.vector.memset(table[s][:, T:], 0.0)
+        b_bf16 = keep.tile([P, SLICES, PAIRS, 2, PACK], BF16, name="b_bf16", align_bytes=64)
         b_words = keep.tile([P, N], U32, name="b_words", align_bytes=64)
         b_scales = keep.tile([P, N], U8, name="b_scales", align_bytes=64)
-        out_v = out.rearrange("(q s b) j -> b q s j", s=S, b=2)
-        zg, ug, d, root, rs = ([None] * S for i in range(5))
+        out_rows = out.rearrange("(q s b) j -> b q s j", s=SLICES, b=2)
 
-        def deal_a():
-            nc.vector.tensor_copy(out=a_words[:].bitcast(I32).rearrange("p (s q) -> p s q", s=S), in_=a_raw[:].bitcast(I32).rearrange("p (q s) -> p s q", s=S))
-            nc.vector.tensor_copy(out=a_scales[:].bitcast(U16).rearrange("p (s q) -> p s q", s=S), in_=a_scales_raw[:].bitcast(U16).rearrange("p (q s) -> p s q", s=S))
+        def round_wb(q0, q1, copy):
+            half = q0 // (PAIRS // 2)
+            first = RUN * q0 - N // 2 * half
+            src = b_raw[half][:, :, first : first + RUN * (q1 - q0)].rearrange("p t (q s b) -> p q s b t", s=SLICES, b=2)
+            copy(out=b_bf16[:, :, q0:q1, :, :].rearrange("p s q b t -> p q s b t"), in_=src)
 
-        def z_product(s):
-            acc = psum.tile([P, T], F32, name=f"zacc{s}", tag=f"acc{s}")
-            nc.tensor.matmul_mx(out=acc[:], lhsT=a_words[:, 2 * P * s : 2 * P * (s + 1)].bitcast(FP4X4), lhsT_scale=a_scales[:, P * s : P * (s + 1)],
-                                rhs=x_words[:].bitcast(FP8X4), rhs_scale=x_scales[:], start=True, stop=True)
-            nc.scalar.copy(out=z[s][:], in_=acc[:])
+        def product(s, weights, weight_scales, tokens, bank, copy):
+            acc = psum.tile([P, tokens.stop - tokens.start], F32, name="acc", tag=bank)
+            nc.tensor.matmul_mx(out=acc[:], lhsT=weights, lhsT_scale=weight_scales[:, P * s : P * (s + 1)],
+                                rhs=x_words[:, tokens].bitcast(FP8X4), rhs_scale=x_scales[:, tokens], start=True, stop=True)
+            copy(out=table[s][:, tokens], in_=acc[:])
 
-        def u_product(s, cols, tag, copy):
-            acc = psum.tile([P, cols.stop - cols.start], F32, name=f"uacc{s}_{cols.start}", tag=tag)
-            nc.tensor.matmul_mx(out=acc[:], lhsT=b_words[:, P * s : P * (s + 1)].bitcast(FP8X4), lhsT_scale=b_scales[:, P * s : P * (s + 1)],
-                                rhs=x_words[:, cols].bitcast(FP8X4), rhs_scale=x_scales[:, cols], start=True, stop=True)
-            copy(out=u[s][:, cols], in_=acc[:])
+        def u_product(s, tokens, bank, copy):
+            product(s, b_words[:, P * s : P * (s + 1)].bitcast(FP8X4), b_scales, tokens, bank, copy)
 
-        def gather(dst, table, offsets):
-            for h in range(J // H):
-                nc.vector.tensor_copy(dst[:, H * h : H * (h + 1)], table[:].indirect(offsets[:, H // 16 * h : H // 16 * (h + 1)]))
+        def z_picked(s):
+            product(s, a_words[:, 2 * P * s : 2 * P * (s + 1)].bitcast(FP4X4), a_scales, slice(0, T), f"bank{s}", nc.scalar.copy)
+            picked = keep.tile([P, J], F32, name=f"z_picked{s}")
+            nc.vector.tensor_copy(picked[:], table[s][:].indirect(list_z[:]))
+            return picked
 
-        def z_gather(s):
-            zg[s] = keep.tile([P, J], F32, name=f"zg{s}")
-            gather(zg[s], z[s], list_z)
+        def on_scalar(name, src, func, bias=0.0):
+            dst = keep.tile(list(src.shape), F32, name=name)
+            nc.scalar.activation(dst[:], src[:], func, bias=bias)
+            return dst
 
-        def cast(q0, q1, copy):
-            half = q0 // 32
-            src = b_raw[half][:, :, 8 * (q0 - 32 * half) : 8 * (q1 - 32 * half)].rearrange("p j (q s b) -> p q s b j", s=S, b=2)
-            copy(out=b_bf[:, :, q0:q1, :, :].rearrange("p s q b j -> p q s b j"), in_=src)
-
-        def quantise(s):
-            nc.vector.quantize_mx(out=b_words[:, P * s : P * (s + 1)].bitcast(FP8X4), scales=b_scales[:, P * s : P * (s + 1)],
-                                  in_=b_bf[:, s, :, :, :].rearrange("p q b j -> p (q b j)"))
-
-        def positive(s, src, width):
-            d[s] = keep.tile([P, width], F32, name=f"d{s}")
-            nc.scalar.activation(d[s][:], src, ACT.Relu)
-
-        def inv_root(s, width):
-            root[s] = keep.tile([P, width], F32, name=f"root{s}")
-            nc.scalar.activation(root[s][:], d[s][:], ACT.Abs_reciprocal_sqrt, bias=1.0)
-
-        def square(s, width):
-            rs[s] = keep.tile([P, width], F32, name=f"rs{s}")
-            nc.scalar.activation(rs[s][:], root[s][:], ACT.Square)
-
-        def finish(s, r):
+        def finish(s, picked, inverse, pieces):
             y = keep.tile([P, J], F32, name=f"y{s}")
-            nc.vector.scalar_tensor_tensor(out=y[:], in0=zg[s][:], scalar=gains[:, 2 * s : 2 * s + 1], in1=r, op0=ALU.mult, op1=ALU.mult)
-            for b in range(2):
-                nc.sync.dma_start(out=out_v[b][:, s, :], in_=y[b:P:2, :])
+            width = J // pieces
+            for piece in range(pieces):
+                slots = slice(width * piece, width * (piece + 1))
+                nc.vector.scalar_tensor_tensor(out=y[:, slots], in0=picked[:, slots], scalar=gains[:, 2 * s : 2 * s + 1],
+                                               in1=inverse[:, slots], op0=ALU.mult, op1=ALU.mult)
+                for b in range(2):
+                    nc.sync.dma_start(out=out_rows[b][:, s, slots], in_=y[b:P:2, slots])
 
-        cast(0, 32, nc.vector.tensor_copy)
-        cast(32, 54, nc.vector.tensor_copy)
-        cast(54, 64, nc.scalar.copy)
-        for s in range(S):
-            quantise(s)
-        deal_a()
-        ug01 = keep.tile([P, 2 * J], F32, name="ug01", tag="a_scales_raw", align_bytes=64)
-        for s in range(S):
-            u_product(s, slice(0, T), f"acc{s}", nc.scalar.copy)
-            ug[s] = ug01[:, J * s : J * (s + 1)] if s < 2 else keep.tile([P, J], F32, name=f"ug{s}")
-            gather(ug[s], u[s], list_u)
-        z_product(0)
-        z_gather(0)
-        positive(0, ug01[:], 2 * J)
-        z_product(1)
-        z_gather(1)
-        inv_root(0, 2 * J)
-        positive(2, ug[2][:], J)
-        square(0, 2 * J)
-        z_product(2)
-        z_gather(2)
-        finish(0, rs[0][:, :J])
-        finish(1, rs[0][:, J:])
-        inv_root(2, J)
-        positive(3, ug[3][:], J)
-        z_product(3)
-        z_gather(3)
-        square(2, J)
-        inv_root(3, J)
-        square(3, J)
-        finish(2, rs[2][:])
-        finish(3, rs[3][:])
+        round_wb(0, PAIRS // 2, nc.vector.tensor_copy)
+        round_wb(PAIRS // 2, VECTOR_ROUNDS_UP_TO, nc.vector.tensor_copy)
+        round_wb(VECTOR_ROUNDS_UP_TO, PAIRS, nc.scalar.copy)
+        for s in range(SLICES):
+            nc.vector.quantize_mx(out=b_words[:, P * s : P * (s + 1)].bitcast(FP8X4), scales=b_scales[:, P * s : P * (s + 1)],
+                                  in_=b_bf16[:, s, :, :, :].rearrange("p q b t -> p (q b t)"))
+
+        nc.vector.tensor_copy(out=a_words[:].bitcast(I32).rearrange("p (s q) -> p s q", s=SLICES),
+                              in_=a_raw[:].bitcast(I32).rearrange("p (q s) -> p s q", s=SLICES))
+        nc.vector.tensor_copy(out=a_scales[:].bitcast(U16).rearrange("p (s q) -> p s q", s=SLICES),
+                              in_=a_scales_raw[:].bitcast(U16).rearrange("p (q s) -> p s q", s=SLICES))
+
+        u_picked01 = keep.tile([P, 2 * J], F32, name="u_picked01", tag="a_scales_raw", align_bytes=64)
+        u_picked = []
+        for s in range(SLICES):
+            if s == 0:
+                u_product(s, slice(0, T // 2), "bank0", nc.scalar.copy)
+                u_product(s, slice(T // 2, T), "spare_bank", nc.vector.tensor_copy)
+            else:
+                u_product(s, slice(0, T), f"bank{s}", nc.scalar.copy)
+            u_picked.append(u_picked01[:, J * s : J * (s + 1)] if s < 2 else keep.tile([P, J], F32, name=f"u_picked{s}"))
+            nc.vector.tensor_copy(u_picked[s][:], table[s][:].indirect(list_u[:]))
+
+        z0 = z_picked(0)
+        positive01 = on_scalar("positive01", u_picked01, ACT.Relu)
+        z1 = z_picked(1)
+        root01 = on_scalar("root01", positive01, ACT.Abs_reciprocal_sqrt, bias=1.0)
+        positive2 = on_scalar("positive2", u_picked[2], ACT.Relu)
+        inverse01 = on_scalar("inverse01", root01, ACT.Square)
+        z2 = z_picked(2)
+        finish(0, z0, inverse01[:, :J], pieces=1)
+        finish(1, z1, inverse01[:, J:], pieces=1)
+        root2 = on_scalar("root2", positive2, ACT.Abs_reciprocal_sqrt, bias=1.0)
+        positive3 = on_scalar("positive3", u_picked[3], ACT.Relu)
+        z3 = z_picked(3)
+        inverse2 = on_scalar("inverse2", root2, ACT.Square)
+        root3 = on_scalar("root3", positive3, ACT.Abs_reciprocal_sqrt, bias=1.0)
+        inverse3 = on_scalar("inverse3", root3, ACT.Square)
+        finish(2, z2, inverse2, pieces=1)
+        finish(3, z3, inverse3, pieces=2)

from contextlib import ExitStack

import concourse.mybir as mybir

K, T, J, N = 512, 512, 512, 512
FLOPS = 2 * 2 * K * N * T

F32 = mybir.dt.float32
BF16 = mybir.dt.bfloat16
I32 = mybir.dt.int32
U32 = mybir.dt.uint32
U16 = mybir.dt.uint16
U8 = mybir.dt.uint8
FP8X4 = mybir.dt.float8_e4m3fn_x4
FP4X4 = mybir.dt.float4_e2m1fn_x4
ACT = mybir.ActivationFunctionType
ALU = mybir.AluOpType

P = 128
PACK = 4
SLICES = N // P
PAIRS = P // 2
RUN = 2 * SLICES
QUADRANTS = 4
VECTOR_ROUNDS_UP_TO = 54


def tile_list_head_divided_by_own_list_kernel(tc, xt_words, xt_scales, wa_words, wa_scales, wb, gm, offs, offs2, out):
    nc = tc.nc
    with ExitStack() as ctx:
        keep = ctx.enter_context(tc.tile_pool(name="keep", bufs=1))
        psum = ctx.enter_context(tc.psum_pool(name="psum", bufs=1))

        list_z = keep.tile([P, J // 16], U16, name="list_z")
        list_u = keep.tile([P, J // 16], U16, name="list_u")
        x_scales = keep.tile([P, T], U8, name="x_scales", align_bytes=64)
        a_scales_raw = keep.tile([P, N], U8, name="a_scales_raw", tag="a_scales_raw", align_bytes=64)
        x_words = keep.tile([P, T], U32, name="x_words", align_bytes=64)
        nc.gpsimd.memset(x_scales[:].bitcast(U32), 0)
        nc.gpsimd.memset(a_scales_raw[:].bitcast(U32), 0)

        warm = keep.tile([P, 1], F32, name="warm")
        warmed = keep.tile([P, 1], F32, name="warmed")
        nc.vector.memset(warm[:], 1.0)
        nc.scalar.activation(warmed[:], warm[:], ACT.Abs_reciprocal_sqrt)

        a_raw = keep.tile([P, 2 * N], U8, name="a_raw", align_bytes=64)
        gains = keep.tile([P, RUN], F32, name="gains")
        b_raw = [keep.tile([P, PACK, N // 2], F32, name=f"b_raw{half}") for half in range(2)]

        def load_scale_rows(queue, src, dst, quad):
            queue.dma_start(out=dst[32 * quad : 32 * quad + 4, :].bitcast(I32), in_=src[0, 4 * quad : 4 * quad + 4, :].bitcast(I32))

        nc.sync.dma_start(list_u[:], offs2)
        nc.sync.dma_start(list_z[:], offs)
        gm_runs = gm.rearrange("(q e) o -> q (e o)", e=RUN)
        for b in range(2):
            nc.sync.dma_start(out=gains[b:P:2, 0 : RUN - 1], in_=gm_runs[:, b : b + RUN - 1])
        nc.sync.dma_start(out=a_raw[:].bitcast(I32), in_=wa_words[0].bitcast(I32))
        wb_rows = wb.rearrange("(p t) n -> p t n", t=PACK)
        for half in range(2):
            nc.sync.dma_start(out=b_raw[half][:], in_=wb_rows[:, :, N // 2 * half : N // 2 * (half + 1)])
        nc.sync.dma_start(out=x_words[:].bitcast(I32), in_=xt_words[0].rearrange("p c t -> p (c t)").bitcast(I32))
        for quad in range(QUADRANTS):
            load_scale_rows(nc.sync, xt_scales, x_scales, quad)
        for quad in range(QUADRANTS):
            load_scale_rows(nc.sync if quad < QUADRANTS // 2 else nc.gpsimd, wa_scales, a_scales_raw, quad)

        a_scales = keep.tile([P, N], U8, name="a_scales", align_bytes=64)
        a_words = keep.tile([P, 2 * N], U8, name="a_words", align_bytes=64)
        table = [keep.tile([P, 2 * T], F32, name=f"table{s}") for s in range(SLICES)]
        for s in range(SLICES):
            nc.vector.memset(table[s][:, T:], 0.0)
        b_bf16 = keep.tile([P, SLICES, PAIRS, 2, PACK], BF16, name="b_bf16", align_bytes=64)
        b_words = keep.tile([P, N], U32, name="b_words", align_bytes=64)
        b_scales = keep.tile([P, N], U8, name="b_scales", align_bytes=64)
        out_rows = out.rearrange("(q s b) j -> b q s j", s=SLICES, b=2)

        def round_wb(q0, q1, copy):
            half = q0 // (PAIRS // 2)
            first = RUN * q0 - N // 2 * half
            src = b_raw[half][:, :, first : first + RUN * (q1 - q0)].rearrange("p t (q s b) -> p q s b t", s=SLICES, b=2)
            copy(out=b_bf16[:, :, q0:q1, :, :].rearrange("p s q b t -> p q s b t"), in_=src)

        def product(s, weights, weight_scales, tokens, bank, copy):
            acc = psum.tile([P, tokens.stop - tokens.start], F32, name="acc", tag=bank)
            nc.tensor.matmul_mx(out=acc[:], lhsT=weights, lhsT_scale=weight_scales[:, P * s : P * (s + 1)],
                                rhs=x_words[:, tokens].bitcast(FP8X4), rhs_scale=x_scales[:, tokens], start=True, stop=True)
            copy(out=table[s][:, tokens], in_=acc[:])

        def u_product(s, tokens, bank, copy):
            product(s, b_words[:, P * s : P * (s + 1)].bitcast(FP8X4), b_scales, tokens, bank, copy)

        def z_picked(s):
            product(s, a_words[:, 2 * P * s : 2 * P * (s + 1)].bitcast(FP4X4), a_scales, slice(0, T), f"bank{s}", nc.scalar.copy)
            picked = keep.tile([P, J], F32, name=f"z_picked{s}")
            nc.vector.tensor_copy(picked[:], table[s][:].indirect(list_z[:]))
            return picked

        def on_scalar(name, src, func, bias=0.0):
            dst = keep.tile(list(src.shape), F32, name=name)
            nc.scalar.activation(dst[:], src[:], func, bias=bias)
            return dst

        def finish(s, picked, inverse, pieces):
            y = keep.tile([P, J], F32, name=f"y{s}")
            width = J // pieces
            for piece in range(pieces):
                slots = slice(width * piece, width * (piece + 1))
                nc.vector.scalar_tensor_tensor(out=y[:, slots], in0=picked[:, slots], scalar=gains[:, 2 * s : 2 * s + 1],
                                               in1=inverse[:, slots], op0=ALU.mult, op1=ALU.mult)
                for b in range(2):
                    nc.sync.dma_start(out=out_rows[b][:, s, slots], in_=y[b:P:2, slots])

        round_wb(0, PAIRS // 2, nc.vector.tensor_copy)
        round_wb(PAIRS // 2, VECTOR_ROUNDS_UP_TO, nc.vector.tensor_copy)
        round_wb(VECTOR_ROUNDS_UP_TO, PAIRS, nc.scalar.copy)
        for s in range(SLICES):
            nc.vector.quantize_mx(out=b_words[:, P * s : P * (s + 1)].bitcast(FP8X4), scales=b_scales[:, P * s : P * (s + 1)],
                                  in_=b_bf16[:, s, :, :, :].rearrange("p q b t -> p (q b t)"))

        nc.vector.tensor_copy(out=a_words[:].bitcast(I32).rearrange("p (s q) -> p s q", s=SLICES),
                              in_=a_raw[:].bitcast(I32).rearrange("p (q s) -> p s q", s=SLICES))
        nc.vector.tensor_copy(out=a_scales[:].bitcast(U16).rearrange("p (s q) -> p s q", s=SLICES),
                              in_=a_scales_raw[:].bitcast(U16).rearrange("p (q s) -> p s q", s=SLICES))

        u_picked01 = keep.tile([P, 2 * J], F32, name="u_picked01", tag="a_scales_raw", align_bytes=64)
        u_picked = []
        for s in range(SLICES):
            if s == 0:
                u_product(s, slice(0, T // 2), "bank0", nc.scalar.copy)
                u_product(s, slice(T // 2, T), "spare_bank", nc.vector.tensor_copy)
            else:
                u_product(s, slice(0, T), f"bank{s}", nc.scalar.copy)
            u_picked.append(u_picked01[:, J * s : J * (s + 1)] if s < 2 else keep.tile([P, J], F32, name=f"u_picked{s}"))
            nc.vector.tensor_copy(u_picked[s][:], table[s][:].indirect(list_u[:]))

        z0 = z_picked(0)
        positive01 = on_scalar("positive01", u_picked01, ACT.Relu)
        z1 = z_picked(1)
        root01 = on_scalar("root01", positive01, ACT.Abs_reciprocal_sqrt, bias=1.0)
        positive2 = on_scalar("positive2", u_picked[2], ACT.Relu)
        inverse01 = on_scalar("inverse01", root01, ACT.Square)
        z2 = z_picked(2)
        finish(0, z0, inverse01[:, :J], pieces=1)
        finish(1, z1, inverse01[:, J:], pieces=1)
        root2 = on_scalar("root2", positive2, ACT.Abs_reciprocal_sqrt, bias=1.0)
        positive3 = on_scalar("positive3", u_picked[3], ACT.Relu)
        z3 = z_picked(3)
        inverse2 = on_scalar("inverse2", root2, ACT.Square)
        root3 = on_scalar("root3", positive3, ACT.Abs_reciprocal_sqrt, bias=1.0)
        inverse3 = on_scalar("inverse3", root3, ACT.Square)
        finish(2, z2, inverse2, pieces=1)
        finish(3, z3, inverse3, pieces=2)
